import numpy as np
import ml_dtypes


def mxq(x, axis, fmt="e4m3"):
    dtype, down = {"e4m3": (ml_dtypes.float8_e4m3fn, 7), "e5m2": (ml_dtypes.float8_e5m2, 14)}[fmt]
    v = np.moveaxis(np.asarray(x, np.float32).astype(ml_dtypes.bfloat16).astype(np.float64), axis, -1)
    blocks = v.reshape(v.shape[:-1] + (-1, 32))
    amax = np.abs(blocks).max(-1, keepdims=True)
    byte = np.maximum(np.where(amax > 0, np.frexp(amax)[1] - 1 + 127, 0) - down, 1)
    scale = np.exp2(byte - 127.0)
    codes = (blocks / scale).astype(np.float32).astype(dtype).astype(np.float64)
    return np.moveaxis((codes * scale).reshape(v.shape), -1, axis)


WIDE = False


def mx_kscale(k):
    if not WIDE:
        return np.ones(k)
    levels = np.array([10, -10, 5, -5, 0])
    if k % 512:
        return np.exp2(np.random.permutation(np.resize(levels, k // 32))).repeat(32)
    a = np.empty((k // 512, 16))
    for p in range(k // 512):
        a[p, :8] = np.random.permutation(np.resize(levels, 8))
        for g in range(8):
            far = levels[np.abs(levels - a[p, g]) >= 10]
            a[p, g + 8] = far[np.random.randint(len(far))]
    return np.exp2(a.ravel()).repeat(32)


def f64(x):
    return np.asarray(x).astype(np.float64)


def striped(idx):
    return np.tile(idx.reshape(-1, 16).T, (8, 1)).astype(np.uint16)


def unstriped(offs):
    return offs[:16].T.reshape(-1).astype(np.int64)


E2M1 = np.array([0.0, 0.5, 1.0, 1.5, 2.0, 3.0, 4.0, 6.0, -0.0, -0.5, -1.0, -1.5, -2.0, -3.0, -4.0, -6.0])


def pack_weight(w, fmt):
    k, n = w.shape
    w = f64(np.asarray(w, np.float32).astype(ml_dtypes.bfloat16)).reshape(k // 32, 32, n)
    amax = np.abs(w).max(1)
    if fmt == "e4m3":
        byte = np.frexp(amax)[1] - 1 + 127 - 7
    else:
        mant, ex = np.frexp(amax / 6.0)
        byte = np.where(mant > 0.5, ex, ex - 1) + 127
    byte = np.clip(np.where(amax > 0, byte, 1), 1, 254)
    scaled = (w * np.exp2(127.0 - byte)[:, None, :]).reshape(k, n).astype(np.float32)
    by_word = np.ascontiguousarray(scaled.reshape(k // 512, 128, 4, n).transpose(0, 1, 3, 2))
    if fmt == "e4m3":
        words = by_word.astype(ml_dtypes.float8_e4m3fn).view(np.uint8)
    else:
        c = by_word.astype(ml_dtypes.float4_e2m1fn).view(np.uint8) & 0xF
        words = (c[..., 0::2] | (c[..., 1::2] << 4)).reshape(k // 512, 128, 2 * n)
    return np.ascontiguousarray(words), np.ascontiguousarray(byte.astype(np.uint8).reshape(k // 512, 16, n))


def unpack_weight(words, scales, fmt):
    g, _, n = scales.shape
    words = np.ascontiguousarray(words).reshape(g, 128, n, -1)
    if fmt == "e4m3":
        vals = words.view(ml_dtypes.float8_e4m3fn).astype(np.float64)
    else:
        nib = np.empty((g, 128, n, 4), np.uint8)
        nib[..., 0::2] = words & 0xF
        nib[..., 1::2] = words >> 4
        vals = E2M1[nib]
    vals = vals * np.repeat(np.exp2(scales.astype(np.float64) - 127.0), 8, axis=1)[..., None]
    return vals.transpose(0, 1, 3, 2).reshape(g * 512, n)


def gelu(v):
    return 0.5 * v * (1.0 + np.tanh(np.sqrt(2.0 / np.pi) * (v + 0.044715 * v**3)))


def striped8(idx):
    return np.concatenate([v.reshape(-1, 16).T for v in idx]).astype(np.uint16)


def unstriped8(offs):
    return np.stack([offs[16 * g:16 * g + 16].T.reshape(-1) for g in range(8)]).astype(np.int64)


def runs(v, idx8):
    k = np.arange(v.shape[0])
    return v[k[:, None], idx8[k % 512 // 64]]


K, T, S, P, H, N = 1536, 4096, 1024, 512, 512, 768


def setup_inputs():
    n = np.random.standard_normal
    ks = mx_kscale(K)[:, None]
    u = mx_kscale(H)[:, None]
    tab_words, tab_scales = pack_weight(n((K, T)) * ks, "e4m3")
    offs = striped(np.random.permutation(T)[:S])
    offs2 = striped8(np.stack([np.random.permutation(S)[:P] for _ in range(8)]))
    w1 = (0.85 * n((K, H)) / np.sqrt(K) / ks).astype(np.float32)
    w2_words, w2_scales = pack_weight(0.85 * n((K, H)) / np.sqrt(K) / ks, "e2m1")
    slope = np.repeat(np.random.uniform(1, 3, H // 64), 64).astype(np.float32)
    share = np.repeat(np.random.uniform(0.1, 0.5, H // 64), 64).astype(np.float32)
    nav = (n((H, P)) * u).astype(np.float32)
    w3 = (3.0 * n((H, N)) / np.sqrt(H) / u).astype(np.float32)
    d = (0.7 * n(N)).astype(np.float32)
    return {"tab_words": tab_words, "tab_scales": tab_scales, "offs": offs, "offs2": offs2,
            "w1": w1, "w2_words": w2_words, "w2_scales": w2_scales,
            "slope": slope, "share": share, "nav": nav, "w3": w3, "d": d}


def reference(tab_words, tab_scales, offs, offs2, w1, w2_words, w2_scales, slope, share, nav, w3, d):
    v = unpack_weight(tab_words, tab_scales, "e4m3")[:, unstriped(offs)]
    w1q = mxq(f64(w1), 0, "e4m3")
    w2q = unpack_weight(w2_words, w2_scales, "e2m1")
    h = np.maximum(w1q.T @ v, w2q.T @ v)
    top = h.max(axis=1)
    hp = runs(h, unstriped8(offs2))
    a = 1.0 / (1.0 + np.exp(-f64(slope)[:, None] * (hp - f64(share)[:, None] * top[:, None])))
    y = mxq(f64(nav) * a, 0, "e4m3")
    w3q = mxq(f64(w3), 0, "e4m3")
    z = (w3q.T @ y) + f64(d)[:, None]
    return np.tanh(z)

@@ -1,0 +1,259 @@
+from contextlib import ExitStack
+
+import concourse.mybir as mybir
+
+K, T, S, M, H, N = 1536, 4096, 1024, 512, 512, 768
+FLOPS = 2 * (2 * K * H * S) + 2 * H * N * M
+
+F32 = mybir.dt.float32
+BF16 = mybir.dt.bfloat16
+I32 = mybir.dt.int32
+U32 = mybir.dt.uint32
+U16 = mybir.dt.uint16
+U8 = mybir.dt.uint8
+FP8X4 = mybir.dt.float8_e4m3fn_x4
+FP4X4 = mybir.dt.float4_e2m1fn_x4
+ACT = mybir.ActivationFunctionType
+ALU = mybir.AluOpType
+AXIS_X = mybir.AxisListType.X
+
+P = 128
+PACK = 4
+PASSES = K // (P * PACK)
+BANK = 512
+HALVES = S // BANK
+CHUNKS = N // P
+MH = M // 2
+
+
+def tile_list_streamer_noise_picker_kernel(
+    tc, tab_words, tab_scales, offs, offs2, w1, w2_words, w2_scales, slope, share, nav, w3, d, out
+):
+    nc = tc.nc
+    with ExitStack() as ctx:
+        sb = ctx.enter_context(tc.tile_pool(name="sb", bufs=1))
+        ps = ctx.enter_context(tc.psum_pool(name="ps", bufs=1))
+
+        def tile(name, shape, dtype):
+            return sb.tile(shape, dtype, name=name, align_bytes=64)
+
+        def bank(name, b, width):
+            return ps.tile([P, width], F32, name=name, tag="bank%d" % b)
+
+        shots = sb.tile([P, S // 16], U16, name="shots")
+        valid = sb.tile([P, M // 16], U16, name="valid")
+        tab = [tile("tab%d" % a, [P, T], U32) for a in range(PASSES)]
+        tab_sc = tile("tab_sc", [P, T], U8)
+        v = [tile("v%d" % a, [P, S], U32) for a in range(PASSES)]
+        v_sc_packed = tile("v_sc_packed", [P, S], U8)
+        v_sc_moved = tile("v_sc_moved", [P, PASSES - 1, S], U8)
+        w2_raw = tile("w2_raw", [P, PASSES, 2 * H], U8)
+        w2_sc_raw = tile("w2_sc_raw", [P, PASSES, H], U8)
+        w2_q = tile("w2_q", [P, PASSES, 2 * H], U8)
+        w2_sc = tile("w2_sc", [P, PASSES, H], U8)
+
+        nc.vector.memset(tab_sc[:].bitcast(I32), 0)
+        nc.vector.memset(w2_sc_raw[:].bitcast(I32), 0)
+        nc.vector.memset(v_sc_moved[:].bitcast(I32), 0)
+
+        nc.sync.dma_start(shots[:], offs)
+        nc.sync.dma_start(w2_raw[:].bitcast(I32), w2_words.rearrange("a p c -> p a c").bitcast(I32))
+        for a in range(PASSES):
+            nc.sync.dma_start(tab[a][:].bitcast(I32), tab_words[a].rearrange("p t i -> p (t i)").bitcast(I32))
+        nc.sync.dma_start(valid[:], offs2)
+        slope_sb = tile("slope_sb", [P, PACK], F32)
+        share_sb = tile("share_sb", [P, PACK], F32)
+        nc.sync.dma_start(slope_sb[:], slope.rearrange("(p i) -> p i", i=PACK))
+        nc.sync.dma_start(share_sb[:], share.rearrange("(p i) -> p i", i=PACK))
+        w1_rows = w1.rearrange("(a p j) c -> a p j c", p=P, j=PACK)
+        w1_pieces = [(a, 0, H) for a in range(PASSES - 1)] + [(PASSES - 1, 0, H // 2), (PASSES - 1, H // 2, H)]
+        w1_raw = []
+        for a, c0, c1 in w1_pieces:
+            raw = tile("w1_raw%d_%d" % (a, c0), [P, PACK, c1 - c0], F32)
+            nc.sync.dma_start(raw[:], w1_rows[a][:, :, c0:c1])
+            w1_raw.append(raw)
+        w3_raw = tile("w3_raw", [P, PACK, N], F32)
+        nc.sync.dma_start(w3_raw[:], w3.rearrange("(p i) n -> p i n", i=PACK))
+        nav_sb = tile("nav_sb", [P, PACK, M], F32)
+        nc.sync.dma_start(nav_sb[:], nav.rearrange("(p i) m -> p i m", i=PACK))
+        d_sb = tile("d_sb", [P, CHUNKS], F32)
+        with nc.allow_non_contiguous_dma(reason="one value of d for each partition and chunk"):
+            nc.sync.dma_start(d_sb[:], d.rearrange("(c p) -> p c", p=P))
+
+        for q in range(4):
+            nc.gpsimd.dma_start(
+                tab_sc[32 * q : 32 * q + 4 * PASSES, :].bitcast(I32),
+                tab_scales[:, 4 * q : 4 * q + 4, :].bitcast(I32),
+            )
+        for q in range(4):
+            nc.gpsimd.dma_start(
+                w2_sc_raw[32 * q : 32 * q + 4, :, :].bitcast(I32),
+                w2_scales[:, 4 * q : 4 * q + 4, :].rearrange("a r c -> r a c").bitcast(I32),
+            )
+
+        nc.vector.tensor_copy(
+            w2_q[:].bitcast(U16).rearrange("p a (i m) -> p a m i", i=PACK),
+            w2_raw[:].bitcast(U16).rearrange("p a (m i) -> p a m i", i=PACK),
+        )
+        nc.vector.tensor_copy(v_sc_packed[:], tab_sc[:].indirect(shots[:]))
+        live = 3 * 32 + 4
+        for a in range(1, PASSES):
+            nc.gpsimd.dma_start(
+                v_sc_moved[0:live, a - 1, :].bitcast(I32), v_sc_packed[4 * a : 4 * a + live, :].bitcast(I32)
+            )
+        v_sc = [v_sc_packed[:]] + [v_sc_moved[:, a - 1, :] for a in range(1, PASSES)]
+        nc.vector.tensor_copy(
+            w2_sc[:].rearrange("p a (i m) -> p a m i", i=PACK),
+            w2_sc_raw[:].rearrange("p a (m i) -> p a m i", i=PACK),
+        )
+
+        h2_ps = {}
+        h2 = {}
+        for a in range(PASSES):
+            if a < PASSES - 1:
+                nc.vector.tensor_copy(v[a][:], tab[a][:].indirect(shots[:]))
+            for s in range(HALVES):
+                cols = slice(s * BANK, (s + 1) * BANK)
+                if a == PASSES - 1:
+                    nc.vector.tensor_copy(
+                        v[a][:, cols], tab[a][:].indirect(shots[:, s * BANK // 16 : (s + 1) * BANK // 16])
+                    )
+                for i in range(PACK):
+                    if a == 0:
+                        h2_ps[i, s] = bank("h2_ps%d_%d" % (i, s), HALVES * i + s, BANK)
+                    nc.tensor.matmul_mx(
+                        out=h2_ps[i, s][:],
+                        lhsT=w2_q[:, a, 2 * P * i : 2 * P * (i + 1)].bitcast(FP4X4),
+                        lhsT_scale=w2_sc[:, a, P * i : P * (i + 1)],
+                        rhs=v[a][:, cols].bitcast(FP8X4),
+                        rhs_scale=v_sc[a][:, cols],
+                        start=(a == 0),
+                        stop=(a == PASSES - 1),
+                    )
+                    if a == PASSES - 1:
+                        h2[i, s] = tile("h2_%d_%d" % (i, s), [P, BANK], F32)
+                        nc.scalar.copy(h2[i, s][:], h2_ps[i, s][:])
+
+        gate_k = tile("gate_k", [P, PACK], F32)
+        nc.vector.scalar_tensor_tensor(gate_k[:], slope_sb[:], -1.0, share_sb[:], ALU.mult, ALU.mult)
+
+        w1_bf = [tile("w1_bf%d" % a, [P, PACK, P, PACK], BF16) for a in range(PASSES)]
+        w1_q = [tile("w1_q%d" % a, [P, H], U32) for a in range(PASSES)]
+        w1_sc = [tile("w1_sc%d" % a, [P, H], U8) for a in range(PASSES)]
+        for (a, c0, c1), raw in zip(w1_pieces, w1_raw):
+            dst = w1_bf[a][:, :, c0 // PACK : c1 // PACK, :].rearrange("p i m j -> p m j i")
+            src = raw[:].rearrange("p j (m i) -> p m j i", i=PACK)
+            if a == PASSES - 1 and c0 == 0:
+                nc.scalar.copy(dst, src)
+            else:
+                nc.vector.tensor_copy(dst, src)
+            if a < PASSES - 1:
+                nc.vector.quantize_mx(
+                    out=w1_q[a][:].bitcast(FP8X4),
+                    scales=w1_sc[a][:],
+                    in_=w1_bf[a][:].rearrange("p i m j -> p (i m j)"),
+                )
+        last = PASSES - 1
+        for i in range(PACK):
+            nc.vector.quantize_mx(
+                out=w1_q[last][:, P * i : P * (i + 1)].bitcast(FP8X4),
+                scales=w1_sc[last][:, P * i : P * (i + 1)],
+                in_=w1_bf[last][:, i].rearrange("p m j -> p (m j)"),
+            )
+
+        h1_ps = {}
+
+        def w1_pass(a, i, s):
+            cols = slice(s * BANK, (s + 1) * BANK)
+            nc.tensor.matmul_mx(
+                out=h1_ps[i, s][:],
+                lhsT=w1_q[a][:, P * i : P * (i + 1)].bitcast(FP8X4),
+                lhsT_scale=w1_sc[a][:, P * i : P * (i + 1)],
+                rhs=v[a][:, cols].bitcast(FP8X4),
+                rhs_scale=v_sc[a][:, cols],
+                start=(a == 0),
+                stop=(a == PASSES - 1),
+            )
+
+        for s in range(HALVES):
+            for i in range(PACK):
+                h1_ps[i, s] = bank("h1_ps%d_%d" % (i, s), HALVES * i + s, BANK)
+                w1_pass(0, i, s)
+
+        w3_bf = tile("w3_bf", [P, N, PACK], BF16)
+        w3_q = tile("w3_q", [P, N], U32)
+        w3_sc = tile("w3_sc", [P, N], U8)
+        gate = tile("gate", [P, PACK, M], F32)
+        top = tile("top", [P, PACK], F32)
+        gate_b = tile("gate_b", [P, PACK], F32)
+
+        def w3_round(c):
+            cols = slice(c * P, (c + 1) * P)
+            nc.scalar.copy(
+                w3_bf[:, cols, :].rearrange("p (g n) i -> p g i n", n=4),
+                w3_raw[:, :, cols].rearrange("p i (g n) -> p g i n", n=4),
+            )
+
+        for i in range(PACK):
+            for a in range(1, PASSES):
+                for s in range(HALVES):
+                    w1_pass(a, i, s)
+            h = tile("h%d" % i, [P, S], F32)
+            for s in range(HALVES):
+                nc.vector.tensor_tensor(h[:, s * BANK : (s + 1) * BANK], h1_ps[i, s][:], h2[i, s][:], ALU.max)
+            nc.vector.tensor_reduce(top[:, i : i + 1], h[:], AXIS_X, ALU.max)
+            nc.vector.tensor_tensor(gate_b[:, i : i + 1], top[:, i : i + 1], gate_k[:, i : i + 1], ALU.mult)
+            cuts = 2 if i == PACK - 1 else 1
+            w = M // cuts
+            for u in range(cuts):
+                nc.scalar.activation(
+                    gate[:, i, u * w : (u + 1) * w],
+                    h[:].indirect(valid[:, u * w // 16 : (u + 1) * w // 16]),
+                    ACT.Sigmoid,
+                    bias=gate_b[:, i : i + 1],
+                    scale=slope_sb[:, i : i + 1],
+                )
+            if i < PACK - 1:
+                w3_round(2 * i)
+                w3_round(2 * i + 1)
+
+        for u in range(2):
+            cols = slice(u * N // 2, (u + 1) * N // 2)
+            nc.vector.quantize_mx(
+                out=w3_q[:, cols].bitcast(FP8X4),
+                scales=w3_sc[:, cols],
+                in_=w3_bf[:, cols, :].rearrange("p n i -> p (n i)"),
+            )
+
+        y_bf = tile("y_bf", [P, M, PACK], BF16)
+        y_q = tile("y_q", [P, M], U32)
+        y_sc = tile("y_sc", [P, M], U8)
+        res = tile("res", [P, CHUNKS, M], F32)
+        out_rows = out.rearrange("(c p) m -> p c m", p=P)
+        for u in range(2):
+            cols = slice(u * MH, (u + 1) * MH)
+            nc.vector.tensor_tensor(
+                y_bf[:, cols, :].rearrange("p (g m) i -> p g i m", m=4),
+                gate[:, :, cols].rearrange("p i (g m) -> p g i m", m=4),
+                nav_sb[:, :, cols].rearrange("p i (g m) -> p g i m", m=4),
+                ALU.mult,
+            )
+            nc.vector.quantize_mx(
+                out=y_q[:, cols].bitcast(FP8X4),
+                scales=y_sc[:, cols],
+                in_=y_bf[:, cols, :].rearrange("p m i -> p (m i)"),
+            )
+            for c in range(CHUNKS):
+                z = bank("z%d_%d" % (u, c), (u * CHUNKS + c) % 8, MH)
+                nc.tensor.matmul_mx(
+                    out=z[:],
+                    lhsT=w3_q[:, P * c : P * (c + 1)].bitcast(FP8X4),
+                    lhsT_scale=w3_sc[:, P * c : P * (c + 1)],
+                    rhs=y_q[:, cols].bitcast(FP8X4),
+                    rhs_scale=y_sc[:, cols],
+                    start=True,
+                    stop=True,
+                )
+                nc.scalar.activation(res[:, c, cols], z[:], ACT.Tanh, bias=d_sb[:, c : c + 1])
+                if c % 2 == 1:
+                    nc.sync.dma_start(out_rows[:, c - 1 : c + 1, cols], res[:, c - 1 : c + 1, cols])

@@ -24,6 +24,7 @@ BANK = 512
 HALVES = S // BANK
 CHUNKS = N // P
 MH = M // 2
+SMALL = 8
 
 
 def tile_list_streamer_noise_picker_kernel(
@@ -34,20 +35,19 @@ def tile_list_streamer_noise_picker_kernel(
         sb = ctx.enter_context(tc.tile_pool(name="sb", bufs=1))
         ps = ctx.enter_context(tc.psum_pool(name="ps", bufs=1))
 
-        def tile(name, shape, dtype):
-            return sb.tile(shape, dtype, name=name, align_bytes=64)
+        def tile(name, shape, dtype, tag=None):
+            return sb.tile(shape, dtype, name=name, tag=tag or name, align_bytes=64)
 
         def bank(name, b, width):
             return ps.tile([P, width], F32, name=name, tag="bank%d" % b)
 
         shots = sb.tile([P, S // 16], U16, name="shots")
         valid = sb.tile([P, M // 16], U16, name="valid")
-        tab = [tile("tab%d" % a, [P, T], U32) for a in range(PASSES)]
-        tab_sc = tile("tab_sc", [P, T], U8)
-        v = [tile("v%d" % a, [P, S], U32) for a in range(PASSES)]
+        tab_sc = tile("tab_sc", [P, T], U8, "ring_c")
+        v = {}
         v_sc_packed = tile("v_sc_packed", [P, S], U8)
         v_sc_moved = tile("v_sc_moved", [P, PASSES - 1, S], U8)
-        w2_raw = tile("w2_raw", [P, PASSES, 2 * H], U8)
+        w2_raw = tile("w2_raw", [P, PASSES, 2 * H], U8, "ring_b")
         w2_sc_raw = tile("w2_sc_raw", [P, PASSES, H], U8)
         w2_q = tile("w2_q", [P, PASSES, 2 * H], U8)
         w2_sc = tile("w2_sc", [P, PASSES, H], U8)
@@ -56,37 +56,27 @@ def tile_list_streamer_noise_picker_kernel(
         nc.vector.memset(w2_sc_raw[:].bitcast(I32), 0)
         nc.vector.memset(v_sc_moved[:].bitcast(I32), 0)
 
-        nc.sync.dma_start(shots[:], offs)
-        nc.sync.dma_start(w2_raw[:].bitcast(I32), w2_words.rearrange("a p c -> p a c").bitcast(I32))
-        for a in range(PASSES):
-            nc.sync.dma_start(tab[a][:].bitcast(I32), tab_words[a].rearrange("p t i -> p (t i)").bitcast(I32))
-        nc.sync.dma_start(valid[:], offs2)
-        slope_sb = tile("slope_sb", [P, PACK], F32)
-        share_sb = tile("share_sb", [P, PACK], F32)
-        nc.sync.dma_start(slope_sb[:], slope.rearrange("(p i) -> p i", i=PACK))
-        nc.sync.dma_start(share_sb[:], share.rearrange("(p i) -> p i", i=PACK))
-        w1_rows = w1.rearrange("(a p j) c -> a p j c", p=P, j=PACK)
-        w1_pieces = [(a, 0, H) for a in range(PASSES - 1)] + [(PASSES - 1, 0, H // 2), (PASSES - 1, H // 2, H)]
-        w1_raw = []
-        for a, c0, c1 in w1_pieces:
-            raw = tile("w1_raw%d_%d" % (a, c0), [P, PACK, c1 - c0], F32)
-            nc.sync.dma_start(raw[:], w1_rows[a][:, :, c0:c1])
-            w1_raw.append(raw)
-        w3_raw = tile("w3_raw", [P, PACK, N], F32)
-        nc.sync.dma_start(w3_raw[:], w3.rearrange("(p i) n -> p i n", i=PACK))
-        nav_sb = tile("nav_sb", [P, PACK, M], F32)
-        nc.sync.dma_start(nav_sb[:], nav.rearrange("(p i) m -> p i m", i=PACK))
-        d_sb = tile("d_sb", [P, CHUNKS], F32)
-        with nc.allow_non_contiguous_dma(reason="one value of d for each partition and chunk"):
-            nc.sync.dma_start(d_sb[:], d.rearrange("(c p) -> p c", p=P))
+        warm_in = tile("warm_in", [P, 1], F32)
+        warm_out = tile("warm_out", [P, 1], F32)
+        nc.vector.memset(warm_in[:], 0.0)
+        nc.scalar.activation(warm_out[:], warm_in[:], ACT.Sigmoid)
 
+        def load_table(a, words):
+            nc.sync.dma_start(words.bitcast(I32), tab_words[a].rearrange("p t i -> p (t i)").bitcast(I32))
+            return words
+
+        nc.sync.dma_start(shots[:], offs)
+        nc.sync.dma_start(valid[:], offs2)
+        nc.sync.dma_start(w2_raw[:].bitcast(I32), w2_words.rearrange("a p c -> p a c").bitcast(I32))
+        tab_first = tile("tab_first", [P, T], U32, "ring_a")
+        tab = [load_table(0, tab_first[:])]
         for q in range(4):
-            nc.gpsimd.dma_start(
+            nc.scalar.dma_start(
                 tab_sc[32 * q : 32 * q + 4 * PASSES, :].bitcast(I32),
                 tab_scales[:, 4 * q : 4 * q + 4, :].bitcast(I32),
             )
         for q in range(4):
-            nc.gpsimd.dma_start(
+            nc.scalar.dma_start(
                 w2_sc_raw[32 * q : 32 * q + 4, :, :].bitcast(I32),
                 w2_scales[:, 4 * q : 4 * q + 4, :].rearrange("a r c -> r a c").bitcast(I32),
             )
@@ -95,10 +85,12 @@ def tile_list_streamer_noise_picker_kernel(
             w2_q[:].bitcast(U16).rearrange("p a (i m) -> p a m i", i=PACK),
             w2_raw[:].bitcast(U16).rearrange("p a (m i) -> p a m i", i=PACK),
         )
+        tab_rest = tile("tab_rest", [P, (PASSES - 1) * T], U32, "ring_b")
+        tab = tab + [load_table(a, tab_rest[:, (a - 1) * T : a * T]) for a in range(1, PASSES)]
         nc.vector.tensor_copy(v_sc_packed[:], tab_sc[:].indirect(shots[:]))
         live = 3 * 32 + 4
         for a in range(1, PASSES):
-            nc.gpsimd.dma_start(
+            nc.scalar.dma_start(
                 v_sc_moved[0:live, a - 1, :].bitcast(I32), v_sc_packed[4 * a : 4 * a + live, :].bitcast(I32)
             )
         v_sc = [v_sc_packed[:]] + [v_sc_moved[:, a - 1, :] for a in range(1, PASSES)]
@@ -110,13 +102,14 @@ def tile_list_streamer_noise_picker_kernel(
         h2_ps = {}
         h2 = {}
         for a in range(PASSES):
+            v[a] = tile("v%d" % a, [P, S], U32, "ring_c" if a == 0 else None)
             if a < PASSES - 1:
-                nc.vector.tensor_copy(v[a][:], tab[a][:].indirect(shots[:]))
+                nc.vector.tensor_copy(v[a][:], tab[a].indirect(shots[:]))
             for s in range(HALVES):
                 cols = slice(s * BANK, (s + 1) * BANK)
                 if a == PASSES - 1:
                     nc.vector.tensor_copy(
-                        v[a][:, cols], tab[a][:].indirect(shots[:, s * BANK // 16 : (s + 1) * BANK // 16])
+                        v[a][:, cols], tab[a].indirect(shots[:, s * BANK // 16 : (s + 1) * BANK // 16])
                     )
                 for i in range(PACK):
                     if a == 0:
@@ -130,19 +123,43 @@ def tile_list_streamer_noise_picker_kernel(
                         start=(a == 0),
                         stop=(a == PASSES - 1),
                     )
-                    if a == PASSES - 1:
-                        h2[i, s] = tile("h2_%d_%d" % (i, s), [P, BANK], F32)
-                        nc.scalar.copy(h2[i, s][:], h2_ps[i, s][:])
+        for i in range(PACK):
+            for s in range(HALVES):
+                h2[i, s] = tile("h2_%d_%d" % (i, s), [P, BANK], F32)
+                nc.scalar.copy(h2[i, s][:], h2_ps[i, s][:])
 
+        w1_rows = w1.rearrange("(a p j) c -> a p j c", p=P, j=PACK)
+        w1_pieces = [(a, 0, H) for a in range(PASSES - 1)] + [(PASSES - 1, 0, H // 2), (PASSES - 1, H // 2, H)]
+        early = tile("early", [P, PASSES * PACK * H], F32, "ring_a")
+        late = tile("late", [P, PACK * (N + M) + 3 * SMALL], F32, "ring_b")
+        w1_raw = []
+        for a, c0, c1 in w1_pieces:
+            raw = early[:, PACK * (a * H + c0) : PACK * (a * H + c1)].rearrange("p (j c) -> p j c", j=PACK)
+            nc.sync.dma_start(raw, w1_rows[a][:, :, c0:c1])
+            w1_raw.append(raw)
+        small = PACK * (N + M)
+        slope_sb = late[:, small : small + PACK]
+        share_sb = late[:, small + SMALL : small + SMALL + PACK]
+        d_sb = late[:, small + 2 * SMALL : small + 2 * SMALL + CHUNKS]
+        nc.sync.dma_start(slope_sb, slope.rearrange("(p i) -> p i", i=PACK))
+        nc.sync.dma_start(share_sb, share.rearrange("(p i) -> p i", i=PACK))
+        gate_s = tile("gate_s", [P, PACK], F32)
         gate_k = tile("gate_k", [P, PACK], F32)
-        nc.vector.scalar_tensor_tensor(gate_k[:], slope_sb[:], -1.0, share_sb[:], ALU.mult, ALU.mult)
+        nc.gpsimd.tensor_tensor(gate_s[:], slope_sb, share_sb, ALU.mult)
+        nc.gpsimd.tensor_scalar(gate_k[:], gate_s[:], -1.0, 0.0, ALU.mult, ALU.add)
+        w3_raw = late[:, : PACK * N].rearrange("p (i n) -> p i n", i=PACK)
+        nc.sync.dma_start(w3_raw, w3.rearrange("(p i) n -> p i n", i=PACK))
+        nav_sb = late[:, PACK * N : small].rearrange("p (i m) -> p i m", i=PACK)
+        nc.sync.dma_start(nav_sb, nav.rearrange("(p i) m -> p i m", i=PACK))
+        with nc.allow_non_contiguous_dma(reason="one value of d for each partition and chunk"):
+            nc.sync.dma_start(d_sb, d.rearrange("(c p) -> p c", p=P))
 
         w1_bf = [tile("w1_bf%d" % a, [P, PACK, P, PACK], BF16) for a in range(PASSES)]
         w1_q = [tile("w1_q%d" % a, [P, H], U32) for a in range(PASSES)]
         w1_sc = [tile("w1_sc%d" % a, [P, H], U8) for a in range(PASSES)]
         for (a, c0, c1), raw in zip(w1_pieces, w1_raw):
             dst = w1_bf[a][:, :, c0 // PACK : c1 // PACK, :].rearrange("p i m j -> p m j i")
-            src = raw[:].rearrange("p j (m i) -> p m j i", i=PACK)
+            src = raw.rearrange("p j (m i) -> p m j i", i=PACK)
             if a == PASSES - 1 and c0 == 0:
                 nc.scalar.copy(dst, src)
             else:
@@ -175,15 +192,12 @@ def tile_list_streamer_noise_picker_kernel(
                 stop=(a == PASSES - 1),
             )
 
-        for s in range(HALVES):
-            for i in range(PACK):
-                h1_ps[i, s] = bank("h1_ps%d_%d" % (i, s), HALVES * i + s, BANK)
-                w1_pass(0, i, s)
-
         w3_bf = tile("w3_bf", [P, N, PACK], BF16)
         w3_q = tile("w3_q", [P, N], U32)
         w3_sc = tile("w3_sc", [P, N], U8)
         gate = tile("gate", [P, PACK, M], F32)
+        y_all = tile("y_all", [P, PACK, M], BF16)
+        y_rows = [y_all[:, i, :] for i in range(PACK)]
         top = tile("top", [P, PACK], F32)
         gate_b = tile("gate_b", [P, PACK], F32)
 
@@ -195,14 +209,16 @@ def tile_list_streamer_noise_picker_kernel(
             )
 
         for i in range(PACK):
-            for a in range(1, PASSES):
+            for s in range(HALVES):
+                h1_ps[i, s] = bank("h1_ps%d_%d" % (i, s), HALVES * i + s, BANK)
+            for a in range(PASSES):
                 for s in range(HALVES):
                     w1_pass(a, i, s)
             h = tile("h%d" % i, [P, S], F32)
             for s in range(HALVES):
                 nc.vector.tensor_tensor(h[:, s * BANK : (s + 1) * BANK], h1_ps[i, s][:], h2[i, s][:], ALU.max)
             nc.vector.tensor_reduce(top[:, i : i + 1], h[:], AXIS_X, ALU.max)
-            nc.vector.tensor_tensor(gate_b[:, i : i + 1], top[:, i : i + 1], gate_k[:, i : i + 1], ALU.mult)
+            nc.vector.tensor_scalar(gate_b[:, i : i + 1], top[:, i : i + 1], gate_k[:, i : i + 1], None, ALU.mult)
             cuts = 2 if i == PACK - 1 else 1
             w = M // cuts
             for u in range(cuts):
@@ -214,6 +230,7 @@ def tile_list_streamer_noise_picker_kernel(
                     scale=slope_sb[:, i : i + 1],
                 )
             if i < PACK - 1:
+                nc.gpsimd.tensor_tensor(y_rows[i], gate[:, i, :], nav_sb[:, i, :], ALU.mult)
                 w3_round(2 * i)
                 w3_round(2 * i + 1)
 
@@ -225,23 +242,24 @@ def tile_list_streamer_noise_picker_kernel(
                 in_=w3_bf[:, cols, :].rearrange("p n i -> p (n i)"),
             )
 
-        y_bf = tile("y_bf", [P, M, PACK], BF16)
         y_q = tile("y_q", [P, M], U32)
         y_sc = tile("y_sc", [P, M], U8)
         res = tile("res", [P, CHUNKS, M], F32)
         out_rows = out.rearrange("(c p) m -> p c m", p=P)
         for u in range(2):
             cols = slice(u * MH, (u + 1) * MH)
+            y_bf = tile("y_bf%d" % u, [P, MH, PACK], BF16, "y_bf")
             nc.vector.tensor_tensor(
-                y_bf[:, cols, :].rearrange("p (g m) i -> p g i m", m=4),
-                gate[:, :, cols].rearrange("p i (g m) -> p g i m", m=4),
-                nav_sb[:, :, cols].rearrange("p i (g m) -> p g i m", m=4),
-                ALU.mult,
+                y_rows[PACK - 1][:, cols], gate[:, PACK - 1, cols], nav_sb[:, PACK - 1, cols], ALU.mult
+            )
+            nc.vector.tensor_copy(
+                y_bf[:].rearrange("p (g m) i -> p g i m", m=4),
+                y_all[:, :, cols].rearrange("p i (g m) -> p g i m", m=4),
             )
             nc.vector.quantize_mx(
                 out=y_q[:, cols].bitcast(FP8X4),
                 scales=y_sc[:, cols],
-                in_=y_bf[:, cols, :].rearrange("p m i -> p (m i)"),
+                in_=y_bf[:].rearrange("p m i -> p (m i)"),
             )
             for c in range(CHUNKS):
                 z = bank("z%d_%d" % (u, c), (u * CHUNKS + c) % 8, MH)

@@ -25,6 +25,7 @@ HALVES = S // BANK
 CHUNKS = N // P
 MH = M // 2
 SMALL = 8
+ROW0 = 16
 
 
 def tile_list_streamer_noise_picker_kernel(
@@ -45,64 +46,66 @@ def tile_list_streamer_noise_picker_kernel(
         valid = sb.tile([P, M // 16], U16, name="valid")
         tab_sc = tile("tab_sc", [P, T], U8, "ring_c")
         v = {}
-        v_sc_packed = tile("v_sc_packed", [P, S], U8)
-        v_sc_moved = tile("v_sc_moved", [P, PASSES - 1, S], U8)
-        w2_raw = tile("w2_raw", [P, PASSES, 2 * H], U8, "ring_b")
-        w2_sc_raw = tile("w2_sc_raw", [P, PASSES, H], U8)
-        w2_q = tile("w2_q", [P, PASSES, 2 * H], U8)
+        v_sc_rows = tile("v_sc_rows", [P, S], U8)
+        w2_sc_rows = tile("w2_sc_rows", [P, H], U8)
+        v_planes = tile("v_planes", [P, PASSES, S], U8)
         w2_sc = tile("w2_sc", [P, PASSES, H], U8)
+        w2_raw = tile("w2_raw", [P, PASSES, 2 * H], U8, "ring_b")
+        w2_sc_raw = tile("w2_sc_raw", [P, H], U8)
+        w2_q = tile("w2_q", [P, PASSES, 2 * H], U8)
 
-        nc.vector.memset(tab_sc[:].bitcast(I32), 0)
-        nc.vector.memset(w2_sc_raw[:].bitcast(I32), 0)
-        nc.vector.memset(v_sc_moved[:].bitcast(I32), 0)
+        for rows in (tab_sc, w2_sc_raw):
+            nc.vector.memset(rows[:ROW0, :].bitcast(I32), 0)
+            nc.vector.memset(rows[ROW0 + 16 * PASSES :, :].bitcast(I32), 0)
+        nc.gpsimd.memset(w2_sc[:].bitcast(I32), 0)
+        nc.gpsimd.memset(v_planes[:].bitcast(I32), 0)
+
+        def load_table(a, tag):
+            words = tile("tab%d" % a, [P, T], U32, tag)[:]
+            nc.sync.dma_start(words.bitcast(I32), tab_words[a].rearrange("p t i -> p (t i)").bitcast(I32))
+            return words
+
+        nc.sync.dma_start(w2_raw[:].bitcast(I32), w2_words.rearrange("a p c -> p a c").bitcast(I32))
+        nc.sync.dma_start(shots[:], offs)
+        for rows, src in ((tab_sc, tab_scales), (w2_sc_raw, w2_scales)):
+            nc.sync.dma_start(
+                rows[ROW0 : ROW0 + 16 * PASSES, :].bitcast(I32), src.rearrange("a q n -> q a n").bitcast(I32)
+            )
+        nc.sync.dma_start(valid[:], offs2)
+        tab = [load_table(0, "ring_a")]
 
         warm_in = tile("warm_in", [P, 1], F32)
         warm_out = tile("warm_out", [P, 1], F32)
         nc.vector.memset(warm_in[:], 0.0)
         nc.scalar.activation(warm_out[:], warm_in[:], ACT.Sigmoid)
 
-        def load_table(a, words):
-            nc.sync.dma_start(words.bitcast(I32), tab_words[a].rearrange("p t i -> p (t i)").bitcast(I32))
-            return words
-
-        nc.sync.dma_start(shots[:], offs)
-        nc.sync.dma_start(valid[:], offs2)
-        nc.sync.dma_start(w2_raw[:].bitcast(I32), w2_words.rearrange("a p c -> p a c").bitcast(I32))
-        tab_first = tile("tab_first", [P, T], U32, "ring_a")
-        tab = [load_table(0, tab_first[:])]
-        for q in range(4):
-            nc.scalar.dma_start(
-                tab_sc[32 * q : 32 * q + 4 * PASSES, :].bitcast(I32),
-                tab_scales[:, 4 * q : 4 * q + 4, :].bitcast(I32),
-            )
-        for q in range(4):
-            nc.scalar.dma_start(
-                w2_sc_raw[32 * q : 32 * q + 4, :, :].bitcast(I32),
-                w2_scales[:, 4 * q : 4 * q + 4, :].rearrange("a r c -> r a c").bitcast(I32),
-            )
-
         nc.vector.tensor_copy(
             w2_q[:].bitcast(U16).rearrange("p a (i m) -> p a m i", i=PACK),
             w2_raw[:].bitcast(U16).rearrange("p a (m i) -> p a m i", i=PACK),
         )
-        tab_rest = tile("tab_rest", [P, (PASSES - 1) * T], U32, "ring_b")
-        tab = tab + [load_table(a, tab_rest[:, (a - 1) * T : a * T]) for a in range(1, PASSES)]
-        nc.vector.tensor_copy(v_sc_packed[:], tab_sc[:].indirect(shots[:]))
-        live = 3 * 32 + 4
-        for a in range(1, PASSES):
-            nc.scalar.dma_start(
-                v_sc_moved[0:live, a - 1, :].bitcast(I32), v_sc_packed[4 * a : 4 * a + live, :].bitcast(I32)
-            )
-        v_sc = [v_sc_packed[:]] + [v_sc_moved[:, a - 1, :] for a in range(1, PASSES)]
+        tab.append(load_table(1, "ring_b"))
+
+        def to_planes(queue, planes, rows):
+            for quad in range(4):
+                queue.dma_start(
+                    planes[32 * quad : 32 * quad + 4].bitcast(I32),
+                    rows[ROW0 + 12 * quad : ROW0 + 12 * quad + 12, :].bitcast(I32),
+                )
+
+        nc.vector.tensor_copy(v_sc_rows[:], tab_sc[:].indirect(shots[:]))
+        to_planes(nc.sync, v_planes, v_sc_rows)
+        tab.append(load_table(2, "ring_c"))
         nc.vector.tensor_copy(
-            w2_sc[:].rearrange("p a (i m) -> p a m i", i=PACK),
-            w2_sc_raw[:].rearrange("p a (m i) -> p a m i", i=PACK),
+            w2_sc_rows[:].rearrange("p (i m) -> p m i", i=PACK),
+            w2_sc_raw[:].rearrange("p (m i) -> p m i", i=PACK),
         )
+        to_planes(nc.scalar, w2_sc, w2_sc_rows)
+        v_sc = [v_planes[:, a, :] for a in range(PASSES)]
 
         h2_ps = {}
         h2 = {}
         for a in range(PASSES):
-            v[a] = tile("v%d" % a, [P, S], U32, "ring_c" if a == 0 else None)
+            v[a] = tile("v%d" % a, [P, S], U32)
             if a < PASSES - 1:
                 nc.vector.tensor_copy(v[a][:], tab[a].indirect(shots[:]))
             for s in range(HALVES):
@@ -123,18 +126,24 @@ def tile_list_streamer_noise_picker_kernel(
                         start=(a == 0),
                         stop=(a == PASSES - 1),
                     )
-        for i in range(PACK):
+
+        def keep_h2(i):
             for s in range(HALVES):
                 h2[i, s] = tile("h2_%d_%d" % (i, s), [P, BANK], F32)
                 nc.scalar.copy(h2[i, s][:], h2_ps[i, s][:])
 
+        keep_h2(0)
+        keep_h2(1)
+
         w1_rows = w1.rearrange("(a p j) c -> a p j c", p=P, j=PACK)
         w1_pieces = [(a, 0, H) for a in range(PASSES - 1)] + [(PASSES - 1, 0, H // 2), (PASSES - 1, H // 2, H)]
-        early = tile("early", [P, PASSES * PACK * H], F32, "ring_a")
-        late = tile("late", [P, PACK * (N + M) + 3 * SMALL], F32, "ring_b")
+        w1_first = tile("w1_first", [P, PACK * H], F32, "ring_a")
+        w1_rest = tile("w1_rest", [P, (PASSES - 1) * PACK * H], F32, "ring_b")
+        late = tile("late", [P, PACK * (N + M) + 3 * SMALL], F32, "ring_c")
         w1_raw = []
         for a, c0, c1 in w1_pieces:
-            raw = early[:, PACK * (a * H + c0) : PACK * (a * H + c1)].rearrange("p (j c) -> p j c", j=PACK)
+            raw = w1_first[:] if a == 0 else w1_rest[:, PACK * ((a - 1) * H + c0) : PACK * ((a - 1) * H + c1)]
+            raw = raw.rearrange("p (j c) -> p j c", j=PACK)
             nc.sync.dma_start(raw, w1_rows[a][:, :, c0:c1])
             w1_raw.append(raw)
         small = PACK * (N + M)
@@ -170,6 +179,8 @@ def tile_list_streamer_noise_picker_kernel(
                     scales=w1_sc[a][:],
                     in_=w1_bf[a][:].rearrange("p i m j -> p (i m j)"),
                 )
+        keep_h2(2)
+        keep_h2(3)
         last = PASSES - 1
         for i in range(PACK):
             nc.vector.quantize_mx(

@@ -47,17 +47,15 @@ def tile_list_streamer_noise_picker_kernel(
         tab_sc = tile("tab_sc", [P, T], U8, "ring_c")
         v = {}
         v_sc_rows = tile("v_sc_rows", [P, S], U8)
-        w2_sc_rows = tile("w2_sc_rows", [P, H], U8)
         v_planes = tile("v_planes", [P, PASSES, S], U8)
         w2_sc = tile("w2_sc", [P, PASSES, H], U8)
         w2_raw = tile("w2_raw", [P, PASSES, 2 * H], U8, "ring_b")
-        w2_sc_raw = tile("w2_sc_raw", [P, H], U8)
+        w2_sc_raw = tile("w2_sc_raw", [P, PASSES, H], U8)
         w2_q = tile("w2_q", [P, PASSES, 2 * H], U8)
 
-        for rows in (tab_sc, w2_sc_raw):
-            nc.vector.memset(rows[:ROW0, :].bitcast(I32), 0)
-            nc.vector.memset(rows[ROW0 + 16 * PASSES :, :].bitcast(I32), 0)
-        nc.gpsimd.memset(w2_sc[:].bitcast(I32), 0)
+        nc.vector.memset(tab_sc[:ROW0, :].bitcast(I32), 0)
+        nc.vector.memset(tab_sc[ROW0 + 16 * PASSES :, :].bitcast(I32), 0)
+        nc.gpsimd.memset(w2_sc_raw[:].bitcast(I32), 0)
         nc.gpsimd.memset(v_planes[:].bitcast(I32), 0)
 
         def load_table(a, tag):
@@ -67,39 +65,33 @@ def tile_list_streamer_noise_picker_kernel(
 
         nc.sync.dma_start(w2_raw[:].bitcast(I32), w2_words.rearrange("a p c -> p a c").bitcast(I32))
         nc.sync.dma_start(shots[:], offs)
-        for rows, src in ((tab_sc, tab_scales), (w2_sc_raw, w2_scales)):
-            nc.sync.dma_start(
-                rows[ROW0 : ROW0 + 16 * PASSES, :].bitcast(I32), src.rearrange("a q n -> q a n").bitcast(I32)
-            )
+        nc.sync.dma_start(
+            tab_sc[ROW0 : ROW0 + 16 * PASSES, :].bitcast(I32), tab_scales.rearrange("a q n -> q a n").bitcast(I32)
+        )
         nc.sync.dma_start(valid[:], offs2)
         tab = [load_table(0, "ring_a")]
-
-        warm_in = tile("warm_in", [P, 1], F32)
-        warm_out = tile("warm_out", [P, 1], F32)
-        nc.vector.memset(warm_in[:], 0.0)
-        nc.scalar.activation(warm_out[:], warm_in[:], ACT.Sigmoid)
+        for quad in range(4):
+            nc.sync.dma_start(
+                w2_sc_raw[32 * quad : 32 * quad + 4].bitcast(I32),
+                w2_scales[:, 4 * quad : 4 * quad + 4, :].rearrange("a r c -> r a c").bitcast(I32),
+            )
 
         nc.vector.tensor_copy(
             w2_q[:].bitcast(U16).rearrange("p a (i m) -> p a m i", i=PACK),
             w2_raw[:].bitcast(U16).rearrange("p a (m i) -> p a m i", i=PACK),
         )
         tab.append(load_table(1, "ring_b"))
-
-        def to_planes(queue, planes, rows):
-            for quad in range(4):
-                queue.dma_start(
-                    planes[32 * quad : 32 * quad + 4].bitcast(I32),
-                    rows[ROW0 + 12 * quad : ROW0 + 12 * quad + 12, :].bitcast(I32),
-                )
-
         nc.vector.tensor_copy(v_sc_rows[:], tab_sc[:].indirect(shots[:]))
-        to_planes(nc.sync, v_planes, v_sc_rows)
+        for quad in range(4):
+            nc.sync.dma_start(
+                v_planes[32 * quad : 32 * quad + 4].bitcast(I32),
+                v_sc_rows[ROW0 + 12 * quad : ROW0 + 12 * quad + 12, :].bitcast(I32),
+            )
         tab.append(load_table(2, "ring_c"))
         nc.vector.tensor_copy(
-            w2_sc_rows[:].rearrange("p (i m) -> p m i", i=PACK),
-            w2_sc_raw[:].rearrange("p (m i) -> p m i", i=PACK),
+            w2_sc[:].rearrange("p a (i m) -> p a m i", i=PACK),
+            w2_sc_raw[:].rearrange("p a (m i) -> p a m i", i=PACK),
         )
-        to_planes(nc.scalar, w2_sc, w2_sc_rows)
         v_sc = [v_planes[:, a, :] for a in range(PASSES)]
 
         h2_ps = {}
@@ -219,6 +211,9 @@ def tile_list_streamer_noise_picker_kernel(
                 w3_raw[:, :, cols].rearrange("p i (g n) -> p g i n", n=4),
             )
 
+        for c in range(CHUNKS):
+            w3_round(c)
+
         for i in range(PACK):
             for s in range(HALVES):
                 h1_ps[i, s] = bank("h1_ps%d_%d" % (i, s), HALVES * i + s, BANK)
@@ -242,8 +237,6 @@ def tile_list_streamer_noise_picker_kernel(
                 )
             if i < PACK - 1:
                 nc.gpsimd.tensor_tensor(y_rows[i], gate[:, i, :], nav_sb[:, i, :], ALU.mult)
-                w3_round(2 * i)
-                w3_round(2 * i + 1)
 
         for u in range(2):
             cols = slice(u * N // 2, (u + 1) * N // 2)

@@ -77,8 +77,8 @@ def tile_list_streamer_noise_picker_kernel(
             )
 
         nc.vector.tensor_copy(
-            w2_q[:].bitcast(U16).rearrange("p a (i m) -> p a m i", i=PACK),
-            w2_raw[:].bitcast(U16).rearrange("p a (m i) -> p a m i", i=PACK),
+            w2_q[:].bitcast(U16).rearrange("p a (i m) -> p a i m", i=PACK),
+            w2_raw[:].bitcast(U16).rearrange("p a (m i) -> p a i m", i=PACK),
         )
         tab.append(load_table(1, "ring_b"))
         nc.vector.tensor_copy(v_sc_rows[:], tab_sc[:].indirect(shots[:]))
@@ -89,8 +89,8 @@ def tile_list_streamer_noise_picker_kernel(
             )
         tab.append(load_table(2, "ring_c"))
         nc.vector.tensor_copy(
-            w2_sc[:].rearrange("p a (i m) -> p a m i", i=PACK),
-            w2_sc_raw[:].rearrange("p a (m i) -> p a m i", i=PACK),
+            w2_sc[:].rearrange("p a (i m) -> p a i m", i=PACK),
+            w2_sc_raw[:].rearrange("p a (m i) -> p a i m", i=PACK),
         )
         v_sc = [v_planes[:, a, :] for a in range(PASSES)]
 
@@ -159,8 +159,8 @@ def tile_list_streamer_noise_picker_kernel(
         w1_q = [tile("w1_q%d" % a, [P, H], U32) for a in range(PASSES)]
         w1_sc = [tile("w1_sc%d" % a, [P, H], U8) for a in range(PASSES)]
         for (a, c0, c1), raw in zip(w1_pieces, w1_raw):
-            dst = w1_bf[a][:, :, c0 // PACK : c1 // PACK, :].rearrange("p i m j -> p m j i")
-            src = raw.rearrange("p j (m i) -> p m j i", i=PACK)
+            dst = w1_bf[a][:, :, c0 // PACK : c1 // PACK, :].rearrange("p i m j -> p m i j")
+            src = raw.rearrange("p j (m i) -> p m i j", i=PACK)
             if a == PASSES - 1 and c0 == 0:
                 nc.scalar.copy(dst, src)
             else:
@@ -199,8 +199,6 @@ def tile_list_streamer_noise_picker_kernel(
         w3_q = tile("w3_q", [P, N], U32)
         w3_sc = tile("w3_sc", [P, N], U8)
         gate = tile("gate", [P, PACK, M], F32)
-        y_all = tile("y_all", [P, PACK, M], BF16)
-        y_rows = [y_all[:, i, :] for i in range(PACK)]
         top = tile("top", [P, PACK], F32)
         gate_b = tile("gate_b", [P, PACK], F32)
 
@@ -235,8 +233,6 @@ def tile_list_streamer_noise_picker_kernel(
                     bias=gate_b[:, i : i + 1],
                     scale=slope_sb[:, i : i + 1],
                 )
-            if i < PACK - 1:
-                nc.gpsimd.tensor_tensor(y_rows[i], gate[:, i, :], nav_sb[:, i, :], ALU.mult)
 
         for u in range(2):
             cols = slice(u * N // 2, (u + 1) * N // 2)
@@ -254,11 +250,10 @@ def tile_list_streamer_noise_picker_kernel(
             cols = slice(u * MH, (u + 1) * MH)
             y_bf = tile("y_bf%d" % u, [P, MH, PACK], BF16, "y_bf")
             nc.vector.tensor_tensor(
-                y_rows[PACK - 1][:, cols], gate[:, PACK - 1, cols], nav_sb[:, PACK - 1, cols], ALU.mult
-            )
-            nc.vector.tensor_copy(
                 y_bf[:].rearrange("p (g m) i -> p g i m", m=4),
-                y_all[:, :, cols].rearrange("p i (g m) -> p g i m", m=4),
+                gate[:, :, cols].rearrange("p i (g m) -> p g i m", m=4),
+                nav_sb[:, :, cols].rearrange("p i (g m) -> p g i m", m=4),
+                ALU.mult,
             )
             nc.vector.quantize_mx(
                 out=y_q[:, cols].bitcast(FP8X4),

from contextlib import ExitStack

import concourse.mybir as mybir

K, T, S, M, H, N = 1536, 4096, 1024, 512, 512, 768
FLOPS = 2 * (2 * K * H * S) + 2 * H * N * M

F32 = mybir.dt.float32
BF16 = mybir.dt.bfloat16
I32 = mybir.dt.int32
U32 = mybir.dt.uint32
U16 = mybir.dt.uint16
U8 = mybir.dt.uint8
FP8X4 = mybir.dt.float8_e4m3fn_x4
FP4X4 = mybir.dt.float4_e2m1fn_x4
ACT = mybir.ActivationFunctionType
ALU = mybir.AluOpType
AXIS_X = mybir.AxisListType.X

P = 128
PACK = 4
PASSES = K // (P * PACK)
BANK = 512
HALVES = S // BANK
CHUNKS = N // P
MH = M // 2
SMALL = 8
ROW0 = 16


def tile_list_streamer_noise_picker_kernel(
    tc, tab_words, tab_scales, offs, offs2, w1, w2_words, w2_scales, slope, share, nav, w3, d, out
):
    nc = tc.nc
    with ExitStack() as ctx:
        sb = ctx.enter_context(tc.tile_pool(name="sb", bufs=1))
        ps = ctx.enter_context(tc.psum_pool(name="ps", bufs=1))

        def tile(name, shape, dtype, tag=None):
            return sb.tile(shape, dtype, name=name, tag=tag or name, align_bytes=64)

        def bank(name, b, width):
            return ps.tile([P, width], F32, name=name, tag="bank%d" % b)

        shots = sb.tile([P, S // 16], U16, name="shots")
        valid = sb.tile([P, M // 16], U16, name="valid")
        tab_sc = tile("tab_sc", [P, T], U8, "ring_c")
        v = {}
        v_sc_rows = tile("v_sc_rows", [P, S], U8)
        v_planes = tile("v_planes", [P, PASSES, S], U8)
        w2_sc = tile("w2_sc", [P, PASSES, H], U8)
        w2_raw = tile("w2_raw", [P, PASSES, 2 * H], U8, "ring_b")
        w2_sc_raw = tile("w2_sc_raw", [P, PASSES, H], U8)
        w2_q = tile("w2_q", [P, PASSES, 2 * H], U8)

        nc.vector.memset(tab_sc[:ROW0, :].bitcast(I32), 0)
        nc.vector.memset(tab_sc[ROW0 + 16 * PASSES :, :].bitcast(I32), 0)
        nc.gpsimd.memset(w2_sc_raw[:].bitcast(I32), 0)
        nc.gpsimd.memset(v_planes[:].bitcast(I32), 0)

        def load_table(a, tag):
            words = tile("tab%d" % a, [P, T], U32, tag)[:]
            nc.sync.dma_start(words.bitcast(I32), tab_words[a].rearrange("p t i -> p (t i)").bitcast(I32))
            return words

        nc.sync.dma_start(w2_raw[:].bitcast(I32), w2_words.rearrange("a p c -> p a c").bitcast(I32))
        nc.sync.dma_start(shots[:], offs)
        nc.sync.dma_start(
            tab_sc[ROW0 : ROW0 + 16 * PASSES, :].bitcast(I32), tab_scales.rearrange("a q n -> q a n").bitcast(I32)
        )
        nc.sync.dma_start(valid[:], offs2)
        tab = [load_table(0, "ring_a")]
        for quad in range(4):
            nc.sync.dma_start(
                w2_sc_raw[32 * quad : 32 * quad + 4].bitcast(I32),
                w2_scales[:, 4 * quad : 4 * quad + 4, :].rearrange("a r c -> r a c").bitcast(I32),
            )

        nc.vector.tensor_copy(
            w2_q[:].bitcast(U16).rearrange("p a (i m) -> p a i m", i=PACK),
            w2_raw[:].bitcast(U16).rearrange("p a (m i) -> p a i m", i=PACK),
        )
        tab.append(load_table(1, "ring_b"))
        nc.vector.tensor_copy(v_sc_rows[:], tab_sc[:].indirect(shots[:]))
        for quad in range(4):
            nc.sync.dma_start(
                v_planes[32 * quad : 32 * quad + 4].bitcast(I32),
                v_sc_rows[ROW0 + 12 * quad : ROW0 + 12 * quad + 12, :].bitcast(I32),
            )
        tab.append(load_table(2, "ring_c"))
        nc.vector.tensor_copy(
            w2_sc[:].rearrange("p a (i m) -> p a i m", i=PACK),
            w2_sc_raw[:].rearrange("p a (m i) -> p a i m", i=PACK),
        )
        v_sc = [v_planes[:, a, :] for a in range(PASSES)]

        h2_ps = {}
        h2 = {}
        for a in range(PASSES):
            v[a] = tile("v%d" % a, [P, S], U32)
            if a < PASSES - 1:
                nc.vector.tensor_copy(v[a][:], tab[a].indirect(shots[:]))
            for s in range(HALVES):
                cols = slice(s * BANK, (s + 1) * BANK)
                if a == PASSES - 1:
                    nc.vector.tensor_copy(
                        v[a][:, cols], tab[a].indirect(shots[:, s * BANK // 16 : (s + 1) * BANK // 16])
                    )
                for i in range(PACK):
                    if a == 0:
                        h2_ps[i, s] = bank("h2_ps%d_%d" % (i, s), HALVES * i + s, BANK)
                    nc.tensor.matmul_mx(
                        out=h2_ps[i, s][:],
                        lhsT=w2_q[:, a, 2 * P * i : 2 * P * (i + 1)].bitcast(FP4X4),
                        lhsT_scale=w2_sc[:, a, P * i : P * (i + 1)],
                        rhs=v[a][:, cols].bitcast(FP8X4),
                        rhs_scale=v_sc[a][:, cols],
                        start=(a == 0),
                        stop=(a == PASSES - 1),
                    )

        def keep_h2(i):
            for s in range(HALVES):
                h2[i, s] = tile("h2_%d_%d" % (i, s), [P, BANK], F32)
                nc.scalar.copy(h2[i, s][:], h2_ps[i, s][:])

        keep_h2(0)
        keep_h2(1)

        w1_rows = w1.rearrange("(a p j) c -> a p j c", p=P, j=PACK)
        w1_pieces = [(a, 0, H) for a in range(PASSES - 1)] + [(PASSES - 1, 0, H // 2), (PASSES - 1, H // 2, H)]
        w1_first = tile("w1_first", [P, PACK * H], F32, "ring_a")
        w1_rest = tile("w1_rest", [P, (PASSES - 1) * PACK * H], F32, "ring_b")
        late = tile("late", [P, PACK * (N + M) + 3 * SMALL], F32, "ring_c")
        w1_raw = []
        for a, c0, c1 in w1_pieces:
            raw = w1_first[:] if a == 0 else w1_rest[:, PACK * ((a - 1) * H + c0) : PACK * ((a - 1) * H + c1)]
            raw = raw.rearrange("p (j c) -> p j c", j=PACK)
            nc.sync.dma_start(raw, w1_rows[a][:, :, c0:c1])
            w1_raw.append(raw)
        small = PACK * (N + M)
        slope_sb = late[:, small : small + PACK]
        share_sb = late[:, small + SMALL : small + SMALL + PACK]
        d_sb = late[:, small + 2 * SMALL : small + 2 * SMALL + CHUNKS]
        nc.sync.dma_start(slope_sb, slope.rearrange("(p i) -> p i", i=PACK))
        nc.sync.dma_start(share_sb, share.rearrange("(p i) -> p i", i=PACK))
        gate_s = tile("gate_s", [P, PACK], F32)
        gate_k = tile("gate_k", [P, PACK], F32)
        nc.gpsimd.tensor_tensor(gate_s[:], slope_sb, share_sb, ALU.mult)
        nc.gpsimd.tensor_scalar(gate_k[:], gate_s[:], -1.0, 0.0, ALU.mult, ALU.add)
        w3_raw = late[:, : PACK * N].rearrange("p (i n) -> p i n", i=PACK)
        nc.sync.dma_start(w3_raw, w3.rearrange("(p i) n -> p i n", i=PACK))
        nav_sb = late[:, PACK * N : small].rearrange("p (i m) -> p i m", i=PACK)
        nc.sync.dma_start(nav_sb, nav.rearrange("(p i) m -> p i m", i=PACK))
        with nc.allow_non_contiguous_dma(reason="one value of d for each partition and chunk"):
            nc.sync.dma_start(d_sb, d.rearrange("(c p) -> p c", p=P))

        w1_bf = [tile("w1_bf%d" % a, [P, PACK, P, PACK], BF16) for a in range(PASSES)]
        w1_q = [tile("w1_q%d" % a, [P, H], U32) for a in range(PASSES)]
        w1_sc = [tile("w1_sc%d" % a, [P, H], U8) for a in range(PASSES)]
        for (a, c0, c1), raw in zip(w1_pieces, w1_raw):
            dst = w1_bf[a][:, :, c0 // PACK : c1 // PACK, :].rearrange("p i m j -> p m i j")
            src = raw.rearrange("p j (m i) -> p m i j", i=PACK)
            if a == PASSES - 1 and c0 == 0:
                nc.scalar.copy(dst, src)
            else:
                nc.vector.tensor_copy(dst, src)
            if a < PASSES - 1:
                nc.vector.quantize_mx(
                    out=w1_q[a][:].bitcast(FP8X4),
                    scales=w1_sc[a][:],
                    in_=w1_bf[a][:].rearrange("p i m j -> p (i m j)"),
                )
        keep_h2(2)
        keep_h2(3)
        last = PASSES - 1
        for i in range(PACK):
            nc.vector.quantize_mx(
                out=w1_q[last][:, P * i : P * (i + 1)].bitcast(FP8X4),
                scales=w1_sc[last][:, P * i : P * (i + 1)],
                in_=w1_bf[last][:, i].rearrange("p m j -> p (m j)"),
            )

        h1_ps = {}

        def w1_pass(a, i, s):
            cols = slice(s * BANK, (s + 1) * BANK)
            nc.tensor.matmul_mx(
                out=h1_ps[i, s][:],
                lhsT=w1_q[a][:, P * i : P * (i + 1)].bitcast(FP8X4),
                lhsT_scale=w1_sc[a][:, P * i : P * (i + 1)],
                rhs=v[a][:, cols].bitcast(FP8X4),
                rhs_scale=v_sc[a][:, cols],
                start=(a == 0),
                stop=(a == PASSES - 1),
            )

        w3_bf = tile("w3_bf", [P, N, PACK], BF16)
        w3_q = tile("w3_q", [P, N], U32)
        w3_sc = tile("w3_sc", [P, N], U8)
        gate = tile("gate", [P, PACK, M], F32)
        top = tile("top", [P, PACK], F32)
        gate_b = tile("gate_b", [P, PACK], F32)

        def w3_round(c):
            cols = slice(c * P, (c + 1) * P)
            nc.scalar.copy(
                w3_bf[:, cols, :].rearrange("p (g n) i -> p g i n", n=4),
                w3_raw[:, :, cols].rearrange("p i (g n) -> p g i n", n=4),
            )

        for c in range(CHUNKS):
            w3_round(c)

        for i in range(PACK):
            for s in range(HALVES):
                h1_ps[i, s] = bank("h1_ps%d_%d" % (i, s), HALVES * i + s, BANK)
            for a in range(PASSES):
                for s in range(HALVES):
                    w1_pass(a, i, s)
            h = tile("h%d" % i, [P, S], F32)
            for s in range(HALVES):
                nc.vector.tensor_tensor(h[:, s * BANK : (s + 1) * BANK], h1_ps[i, s][:], h2[i, s][:], ALU.max)
            nc.vector.tensor_reduce(top[:, i : i + 1], h[:], AXIS_X, ALU.max)
            nc.vector.tensor_scalar(gate_b[:, i : i + 1], top[:, i : i + 1], gate_k[:, i : i + 1], None, ALU.mult)
            cuts = 2 if i == PACK - 1 else 1
            w = M // cuts
            for u in range(cuts):
                nc.scalar.activation(
                    gate[:, i, u * w : (u + 1) * w],
                    h[:].indirect(valid[:, u * w // 16 : (u + 1) * w // 16]),
                    ACT.Sigmoid,
                    bias=gate_b[:, i : i + 1],
                    scale=slope_sb[:, i : i + 1],
                )

        for u in range(2):
            cols = slice(u * N // 2, (u + 1) * N // 2)
            nc.vector.quantize_mx(
                out=w3_q[:, cols].bitcast(FP8X4),
                scales=w3_sc[:, cols],
                in_=w3_bf[:, cols, :].rearrange("p n i -> p (n i)"),
            )

        y_q = tile("y_q", [P, M], U32)
        y_sc = tile("y_sc", [P, M], U8)
        res = tile("res", [P, CHUNKS, M], F32)
        out_rows = out.rearrange("(c p) m -> p c m", p=P)
        for u in range(2):
            cols = slice(u * MH, (u + 1) * MH)
            y_bf = tile("y_bf%d" % u, [P, MH, PACK], BF16, "y_bf")
            nc.vector.tensor_tensor(
                y_bf[:].rearrange("p (g m) i -> p g i m", m=4),
                gate[:, :, cols].rearrange("p i (g m) -> p g i m", m=4),
                nav_sb[:, :, cols].rearrange("p i (g m) -> p g i m", m=4),
                ALU.mult,
            )
            nc.vector.quantize_mx(
                out=y_q[:, cols].bitcast(FP8X4),
                scales=y_sc[:, cols],
                in_=y_bf[:].rearrange("p m i -> p (m i)"),
            )
            for c in range(CHUNKS):
                z = bank("z%d_%d" % (u, c), (u * CHUNKS + c) % 8, MH)
                nc.tensor.matmul_mx(
                    out=z[:],
                    lhsT=w3_q[:, P * c : P * (c + 1)].bitcast(FP8X4),
                    lhsT_scale=w3_sc[:, P * c : P * (c + 1)],
                    rhs=y_q[:, cols].bitcast(FP8X4),
                    rhs_scale=y_sc[:, cols],
                    start=True,
                    stop=True,
                )
                nc.scalar.activation(res[:, c, cols], z[:], ACT.Tanh, bias=d_sb[:, c : c + 1])
                if c % 2 == 1:
                    nc.sync.dma_start(out_rows[:, c - 1 : c + 1, cols], res[:, c - 1 : c + 1, cols])
